import numpy as np
import ml_dtypes


def mxq(x, axis, fmt="e4m3"):
    dtype, down = {"e4m3": (ml_dtypes.float8_e4m3fn, 7), "e5m2": (ml_dtypes.float8_e5m2, 14)}[fmt]
    v = np.moveaxis(np.asarray(x, np.float32).astype(ml_dtypes.bfloat16).astype(np.float64), axis, -1)
    blocks = v.reshape(v.shape[:-1] + (-1, 32))
    amax = np.abs(blocks).max(-1, keepdims=True)
    byte = np.maximum(np.where(amax > 0, np.frexp(amax)[1] - 1 + 127, 0) - down, 1)
    scale = np.exp2(byte - 127.0)
    codes = (blocks / scale).astype(np.float32).astype(dtype).astype(np.float64)
    return np.moveaxis((codes * scale).reshape(v.shape), -1, axis)


WIDE = False


def mx_kscale(k, group=512):
    if not WIDE:
        return np.ones(k)
    levels = np.array([10, -10, 5, -5, 0])
    if group != 512:
        return np.exp2(np.random.permutation(np.resize(levels, k // group))).repeat(group)
    if k % 512:
        return np.exp2(np.random.permutation(np.resize(levels, k // 32))).repeat(32)
    a = np.empty((k // 512, 16))
    for p in range(k // 512):
        a[p, :8] = np.random.permutation(np.resize(levels, 8))
        for g in range(8):
            far = levels[np.abs(levels - a[p, g]) >= 10]
            a[p, g + 8] = far[np.random.randint(len(far))]
    return np.exp2(a.ravel()).repeat(32)


def f64(x):
    return np.asarray(x).astype(np.float64)


def striped(idx):
    return np.tile(np.asarray(idx).reshape(-1, 16).T, (8, 1)).astype(np.uint16)


def unstriped(offs):
    return offs[:16].T.reshape(-1).astype(np.int64)


H, KV, D, NQ, N = 4, 4, 128, 512, 512


def setup_inputs():
    n = np.random.standard_normal
    s = mx_kscale(D, 0)[:, None]
    u = mx_kscale(N)
    t = np.random.uniform(0.5, 2.0, N) * u
    v = n((KV, N, 128))
    v[:, :, 127] = 1.0
    return {
        "qT": (n((H, D, NQ)) * s * (0.70 / np.sqrt(D))).astype(np.float32),
        "kT": (n((KV, D, N)) / s).astype(np.float32),
        "t": t.reshape(N, 1).astype(np.float32),
        "v": (v / t[:, None]).astype(np.float32),
        "mask": (np.arange(N)[:, None] <= np.sort(np.random.randint(N // 4, N, NQ))[None, :]).astype(np.float32),
    }


def reference(qT, kT, t, v, mask):
    a = mxq(f64(kT), 1, "e4m3").transpose(0, 2, 1) @ mxq(f64(qT), 1, "e4m3")
    p = np.exp(a)
    p = p * f64(mask)
    w = p * f64(t)
    y = mxq(w, 1, "e4m3").transpose(0, 2, 1) @ mxq(f64(v), 1, "e4m3")
    y = y / (y[:, :, 127:128])
    return y

@@ -1,0 +1,258 @@
+from contextlib import ExitStack
+
+import concourse.mybir as mybir
+
+H, D, NQ, N = 4, 128, 512, 512
+FLOPS = 2 * 2 * H * D * NQ * N
+
+F32 = mybir.dt.float32
+BF16 = mybir.dt.bfloat16
+U32 = mybir.dt.uint32
+U8 = mybir.dt.uint8
+FP8X4 = mybir.dt.float8_e4m3fn_x4
+ACT = mybir.ActivationFunctionType
+ALU = mybir.AluOpType
+
+P = 128
+PACK = 4
+ROWS = 32
+QB = 128
+BLOCKS = NQ // QB
+
+
+def tile_rows_mask_kernel(tc, qT, kT, t, v, mask, out):
+    nc = tc.nc
+    with ExitStack() as ctx:
+        sb = ctx.enter_context(tc.tile_pool(name="sb", bufs=1))
+        ps = ctx.enter_context(tc.psum_pool(name="ps", bufs=1))
+        ctx.enter_context(tc.manual_schedule())
+
+        def tile(name, shape, dtype):
+            return sb.tile(shape, dtype, name=name, align_bytes=64)
+
+        def mx_tiles(name, words):
+            return tile(name + "_codes", [P, words], U32), tile(name + "_scales", [P, words], U8)
+
+        def quantize(mx, first, words, values):
+            cols = slice(first, first + words)
+            nc.vector.quantize_mx(out=mx[0][:, cols].bitcast(FP8X4), scales=mx[1][:, cols], in_=values)
+
+        q_rows = qT.rearrange("h (p j) n -> (h p) j n", j=PACK)
+        k_rows = kT.rearrange("h (p j) n -> (h p) j n", j=PACK)
+        m_rows = mask.rearrange("(p r) n -> p r n", r=PACK)
+        v_rows = v.rearrange("h (p r) e -> p h (r e)", r=PACK)
+
+        def load(name, rows, first, width):
+            raw = tile(name, [P, PACK, width], F32)
+            nc.sync.dma_start(out=raw[:], in_=rows[:, :, first : first + width])
+            return raw
+
+        def load_v(pair):
+            raw = tile("v_raw%d" % pair, [P, 2, PACK * D], F32)
+            nc.sync.dma_start(out=raw[:], in_=v_rows[:, 2 * pair : 2 * pair + 2, :])
+            return raw
+
+        t_sb = tile("t_sb", [P, PACK], F32)
+        nc.scalar.dma_start(out=t_sb[:], in_=t.rearrange("(p r) o -> p (r o)", r=PACK))
+        k_raw = [load("k_raw0", k_rows, 0, 256)]
+        q_raw = [load("q_raw0", q_rows, 0, QB)[:]]
+        k_raw.append(load("k_raw1", k_rows, 256, 256))
+        m_raw = [load("m_raw0", m_rows, 0, QB)]
+        q_raw.append(load("q_raw1", q_rows, QB, QB)[:])
+        m_raw.append(load("m_raw1", m_rows, QB, QB))
+        v_raw = [load_v(0), load_v(1)]
+        q_late = load("q_raw2", q_rows, 2 * QB, 2 * QB)
+        q_raw.extend([q_late[:, :, 0:QB], q_late[:, :, QB : 2 * QB]])
+        m_raw.append(load("m_raw2", m_rows, 2 * QB, 2 * QB))
+
+        score_bank = [ps.tile([P, PACK, QB], F32, name="score%d" % h) for h in range(H)]
+        y_bank = [ps.tile([P, H, D], F32, name="y%d" % b) for b in range(BLOCKS)]
+
+        k_mx = [mx_tiles("k%d" % r, P) for r in range(PACK)]
+        q_mx = [mx_tiles("q%d" % b, QB) for b in range(BLOCKS)]
+        v_mx = [mx_tiles("v%d" % pair, 2 * D) for pair in range(2)]
+        k_bf = [tile("k_bf%d" % half, [P, PACK, 64, PACK], BF16) for half in range(2)]
+        q_bf = [tile("q_bf%d" % b, [P, QB, PACK], BF16) for b in range(BLOCKS)]
+        v_bf = [tile("v_bf%d" % pair, [P, 2, D, PACK], BF16) for pair in range(2)]
+        mt = [tile("mt%d" % i, [P, PACK, w], F32) for i, w in enumerate((QB, QB, 2 * QB))]
+        mt_of = [mt[0][:], mt[1][:], mt[2][:, :, 0:QB], mt[2][:, :, QB : 2 * QB]]
+        p_sb = {(b, h): tile("p%d%d" % (b, h), [P, PACK * QB], F32) for b in range(BLOCKS) for h in range(H)}
+        w_bf = {(b, pair): tile("w%d%d" % (b, pair), [P, 2, PACK * QB], BF16) for b in range(BLOCKS) for pair in range(2)}
+        w_mx = {(b, pair): mx_tiles("w%d%d" % (b, pair), 2 * QB) for b in range(BLOCKS) for pair in range(2)}
+        inv = [tile("inv%d" % b, [P, H], F32) for b in range(BLOCKS)]
+        res = [tile("res%d" % b, [P, H, D], F32) for b in range(BLOCKS)]
+
+        def pack_k(half):
+            nc.vector.tensor_copy(
+                out=k_bf[half][:].rearrange("p r s j -> p s j r"),
+                in_=k_raw[half][:].rearrange("p j (s r) -> p s j r", r=PACK),
+            )
+
+        def quant_k(half):
+            for r in range(PACK):
+                quantize(k_mx[r], 64 * half, 64, k_bf[half][:, r].rearrange("p s j -> p (s j)"))
+
+        def pack_q(b):
+            nc.vector.tensor_copy(
+                out=q_bf[b][:].rearrange("p (c i) j -> p c j i", i=4),
+                in_=q_raw[b].rearrange("p j (c i) -> p c j i", i=4),
+            )
+
+        def quant_q(b):
+            quantize(q_mx[b], 0, QB, q_bf[b][:].rearrange("p n j -> p (n j)"))
+
+        def pack_v(pair):
+            nc.scalar.copy(
+                out=v_bf[pair][:].rearrange("p h (c i) r -> p h c r i", i=4),
+                in_=v_raw[pair][:].rearrange("p h (r c i) -> p h c r i", r=PACK, i=4),
+            )
+
+        def quant_v(pair):
+            quantize(v_mx[pair], 0, 2 * D, v_bf[pair][:].rearrange("p h e r -> p (h e r)"))
+
+        def mask_times_t(i):
+            for r in range(PACK):
+                nc.vector.tensor_scalar(
+                    out=mt[i][:, r, :], in0=m_raw[i][:, r, :], scalar1=t_sb[:, r : r + 1], scalar2=None, op0=ALU.mult
+                )
+
+        def scores(b, h):
+            rows = slice(ROWS * h, ROWS * (h + 1))
+            for r in range(PACK):
+                nc.tensor.matmul_mx(
+                    out=score_bank[h][:, r, :],
+                    lhsT=k_mx[r][0][rows, :].bitcast(FP8X4),
+                    lhsT_scale=k_mx[r][1][rows, :],
+                    rhs=q_mx[b][0][rows, :].bitcast(FP8X4),
+                    rhs_scale=q_mx[b][1][rows, :],
+                    start=True,
+                    stop=True,
+                )
+
+        def exp(b, h):
+            nc.scalar.activation(
+                out=p_sb[b, h][:].rearrange("p (c r i) -> p c r i", r=PACK, i=2),
+                in_=score_bank[h][:].rearrange("p r (c i) -> p c r i", i=2),
+                func=ACT.Exp,
+            )
+
+        def weigh(b, h):
+            nc.vector.tensor_tensor(
+                out=w_bf[b, h // 2][:, h % 2, :].rearrange("p (c i r) -> p c r i", r=PACK, i=2),
+                in0=p_sb[b, h][:].rearrange("p (c r i) -> p c r i", r=PACK, i=2),
+                in1=mt_of[b].rearrange("p r (c i) -> p c r i", i=2),
+                op=ALU.mult,
+            )
+
+        def quant_w(b, first, count):
+            values = w_bf[b, first // 2][:].rearrange("p h n -> p (h n)")
+            start = (first % 2) * PACK * QB
+            quantize(w_mx[b, first // 2], (first % 2) * QB, count * QB, values[:, start : start + count * PACK * QB])
+
+        def y_of(b, h):
+            bank = (b + max(h - 1, 0)) % BLOCKS if b == BLOCKS - 1 else b
+            return y_bank[bank][:, h, :]
+
+        def mix(b, h):
+            cols = slice((h % 2) * QB, (h % 2 + 1) * QB)
+            nc.tensor.matmul_mx(
+                out=y_of(b, h),
+                lhsT=w_mx[b, h // 2][0][:, cols].bitcast(FP8X4),
+                lhsT_scale=w_mx[b, h // 2][1][:, cols],
+                rhs=v_mx[h // 2][0][:, cols].bitcast(FP8X4),
+                rhs_scale=v_mx[h // 2][1][:, cols],
+                start=True,
+                stop=True,
+            )
+
+        def invert(b, first, count):
+            if count == 1:
+                src = y_of(b, first)[:, D - 1 : D]
+            else:
+                src = y_bank[b][:, first : first + count, D - 1]
+            nc.vector.reciprocal(out=inv[b][:, first : first + count], in_=src)
+
+        def divide(b, first, count):
+            for h in range(first, first + count):
+                nc.scalar.activation(out=res[b][:, h, :], in_=y_of(b, h), func=ACT.Copy, scale=inv[b][:, h : h + 1])
+            heads = slice(first, first + count)
+            nc.sync.dma_start(
+                out=out[heads, QB * b : QB * (b + 1), :].rearrange("h q e -> q h e"), in_=res[b][:, heads, :]
+            )
+
+        def scores_exp(b):
+            for h in range(H):
+                scores(b, h)
+                exp(b, h)
+
+        def mix_block(b):
+            for h in range(H):
+                mix(b, h)
+
+        pack_k(0)
+        pack_q(0)
+        quant_k(0)
+        quant_q(0)
+        pack_k(1)
+        quant_k(1)
+        scores_exp(0)
+        mask_times_t(0)
+        pack_q(1)
+        weigh(0, 0)
+        quant_q(1)
+        scores_exp(1)
+        pack_v(0)
+        pack_v(1)
+        weigh(0, 1)
+        weigh(0, 2)
+        quant_w(0, 0, 2)
+        weigh(0, 3)
+        mask_times_t(1)
+        quant_w(0, 2, 2)
+        weigh(1, 0)
+        pack_q(2)
+        weigh(1, 1)
+        quant_q(2)
+        scores_exp(2)
+        weigh(1, 2)
+        quant_w(1, 0, 2)
+        pack_q(3)
+        weigh(1, 3)
+        quant_q(3)
+        quant_v(0)
+        quant_w(1, 2, 2)
+        mask_times_t(2)
+        quant_v(1)
+        mix_block(0)
+        mix_block(1)
+        weigh(2, 0)
+        invert(0, 0, H)
+        divide(0, 0, H)
+        weigh(2, 1)
+        invert(1, 0, H)
+        scores_exp(3)
+        divide(1, 0, H)
+        weigh(2, 2)
+        quant_w(2, 0, 2)
+        weigh(2, 3)
+        weigh(3, 0)
+        quant_w(2, 2, 2)
+        mix_block(2)
+        weigh(3, 1)
+        invert(2, 0, H)
+        divide(2, 0, H)
+        weigh(3, 2)
+        quant_w(3, 0, 2)
+        mix(3, 0)
+        mix(3, 1)
+        weigh(3, 3)
+        quant_w(3, 2, 1)
+        mix(3, 2)
+        invert(3, 0, 2)
+        divide(3, 0, 2)
+        quant_w(3, 3, 1)
+        mix(3, 3)
+        invert(3, 2, 1)
+        divide(3, 2, 1)
+        invert(3, 3, 1)
+        divide(3, 3, 1)

@@ -42,9 +42,9 @@ def tile_rows_mask_kernel(tc, qT, kT, t, v, mask, out):
         m_rows = mask.rearrange("(p r) n -> p r n", r=PACK)
         v_rows = v.rearrange("h (p r) e -> p h (r e)", r=PACK)
 
-        def load(name, rows, first, width):
-            raw = tile(name, [P, PACK, width], F32)
-            nc.sync.dma_start(out=raw[:], in_=rows[:, :, first : first + width])
+        def load(name, rows, first, count):
+            raw = tile(name, [P, count, NQ], F32)
+            nc.sync.dma_start(out=raw[:], in_=rows[:, first : first + count, :])
             return raw
 
         def load_v(pair):
@@ -54,16 +54,11 @@ def tile_rows_mask_kernel(tc, qT, kT, t, v, mask, out):
 
         t_sb = tile("t_sb", [P, PACK], F32)
         nc.scalar.dma_start(out=t_sb[:], in_=t.rearrange("(p r) o -> p (r o)", r=PACK))
-        k_raw = [load("k_raw0", k_rows, 0, 256)]
-        q_raw = [load("q_raw0", q_rows, 0, QB)[:]]
-        k_raw.append(load("k_raw1", k_rows, 256, 256))
-        m_raw = [load("m_raw0", m_rows, 0, QB)]
-        q_raw.append(load("q_raw1", q_rows, QB, QB)[:])
-        m_raw.append(load("m_raw1", m_rows, QB, QB))
+        k_raw = load("k_raw", k_rows, 0, PACK)
+        q_raw = load("q_raw", q_rows, 0, PACK)
+        m_first = load("m_raw0", m_rows, 0, 2)
+        m_raw = [m_first[:, 0, :], m_first[:, 1, :], load("m_raw2", m_rows, 2, 1)[:, 0, :], load("m_raw3", m_rows, 3, 1)[:, 0, :]]
         v_raw = [load_v(0), load_v(1)]
-        q_late = load("q_raw2", q_rows, 2 * QB, 2 * QB)
-        q_raw.extend([q_late[:, :, 0:QB], q_late[:, :, QB : 2 * QB]])
-        m_raw.append(load("m_raw2", m_rows, 2 * QB, 2 * QB))
 
         score_bank = [ps.tile([P, PACK, QB], F32, name="score%d" % h) for h in range(H)]
         y_bank = [ps.tile([P, H, D], F32, name="y%d" % b) for b in range(BLOCKS)]
@@ -71,50 +66,45 @@ def tile_rows_mask_kernel(tc, qT, kT, t, v, mask, out):
         k_mx = [mx_tiles("k%d" % r, P) for r in range(PACK)]
         q_mx = [mx_tiles("q%d" % b, QB) for b in range(BLOCKS)]
         v_mx = [mx_tiles("v%d" % pair, 2 * D) for pair in range(2)]
-        k_bf = [tile("k_bf%d" % half, [P, PACK, 64, PACK], BF16) for half in range(2)]
+        k_bf = [tile("k_bf%d" % half, [P, 2, P, PACK], BF16) for half in range(2)]
         q_bf = [tile("q_bf%d" % b, [P, QB, PACK], BF16) for b in range(BLOCKS)]
         v_bf = [tile("v_bf%d" % pair, [P, 2, D, PACK], BF16) for pair in range(2)]
-        mt = [tile("mt%d" % i, [P, PACK, w], F32) for i, w in enumerate((QB, QB, 2 * QB))]
-        mt_of = [mt[0][:], mt[1][:], mt[2][:, :, 0:QB], mt[2][:, :, QB : 2 * QB]]
+        mt = tile("mt", [P, PACK, NQ], F32)
         p_sb = {(b, h): tile("p%d%d" % (b, h), [P, PACK * QB], F32) for b in range(BLOCKS) for h in range(H)}
         w_bf = {(b, pair): tile("w%d%d" % (b, pair), [P, 2, PACK * QB], BF16) for b in range(BLOCKS) for pair in range(2)}
         w_mx = {(b, pair): mx_tiles("w%d%d" % (b, pair), 2 * QB) for b in range(BLOCKS) for pair in range(2)}
         inv = [tile("inv%d" % b, [P, H], F32) for b in range(BLOCKS)]
         res = [tile("res%d" % b, [P, H, D], F32) for b in range(BLOCKS)]
 
-        def pack_k(half):
-            nc.vector.tensor_copy(
+        def pack_k(copy, half):
+            copy(
                 out=k_bf[half][:].rearrange("p r s j -> p s j r"),
-                in_=k_raw[half][:].rearrange("p j (s r) -> p s j r", r=PACK),
+                in_=k_raw[:].rearrange("p j (s r) -> p s j r", r=PACK)[:, :, :, 2 * half : 2 * half + 2],
             )
 
-        def quant_k(half):
-            for r in range(PACK):
-                quantize(k_mx[r], 64 * half, 64, k_bf[half][:, r].rearrange("p s j -> p (s j)"))
+        def quant_k(r):
+            quantize(k_mx[r], 0, P, k_bf[r // 2][:, r % 2].rearrange("p s j -> p (s j)"))
 
-        def pack_q(b):
-            nc.vector.tensor_copy(
+        def pack_q(copy, b):
+            copy(
                 out=q_bf[b][:].rearrange("p (c i) j -> p c j i", i=4),
-                in_=q_raw[b].rearrange("p j (c i) -> p c j i", i=4),
+                in_=q_raw[:, :, QB * b : QB * (b + 1)].rearrange("p j (c i) -> p c j i", i=4),
             )
 
         def quant_q(b):
             quantize(q_mx[b], 0, QB, q_bf[b][:].rearrange("p n j -> p (n j)"))
 
-        def pack_v(pair):
+        def pack_v(h):
             nc.scalar.copy(
-                out=v_bf[pair][:].rearrange("p h (c i) r -> p h c r i", i=4),
-                in_=v_raw[pair][:].rearrange("p h (r c i) -> p h c r i", r=PACK, i=4),
+                out=v_bf[h // 2][:, h % 2].rearrange("p (c i) r -> p c r i", i=4),
+                in_=v_raw[h // 2][:, h % 2, :].rearrange("p (r c i) -> p c r i", r=PACK, i=4),
             )
 
         def quant_v(pair):
             quantize(v_mx[pair], 0, 2 * D, v_bf[pair][:].rearrange("p h e r -> p (h e r)"))
 
-        def mask_times_t(i):
-            for r in range(PACK):
-                nc.vector.tensor_scalar(
-                    out=mt[i][:, r, :], in0=m_raw[i][:, r, :], scalar1=t_sb[:, r : r + 1], scalar2=None, op0=ALU.mult
-                )
+        def mask_times_t(r):
+            nc.vector.tensor_scalar(out=mt[:, r, :], in0=m_raw[r], scalar1=t_sb[:, r : r + 1], scalar2=None, op0=ALU.mult)
 
         def scores(b, h):
             rows = slice(ROWS * h, ROWS * (h + 1))
@@ -140,7 +130,7 @@ def tile_rows_mask_kernel(tc, qT, kT, t, v, mask, out):
             nc.vector.tensor_tensor(
                 out=w_bf[b, h // 2][:, h % 2, :].rearrange("p (c i r) -> p c r i", r=PACK, i=2),
                 in0=p_sb[b, h][:].rearrange("p (c r i) -> p c r i", r=PACK, i=2),
-                in1=mt_of[b].rearrange("p r (c i) -> p c r i", i=2),
+                in1=mt[:, :, QB * b : QB * (b + 1)].rearrange("p r (c i) -> p c r i", i=2),
                 op=ALU.mult,
             )
 
@@ -189,55 +179,58 @@ def tile_rows_mask_kernel(tc, qT, kT, t, v, mask, out):
             for h in range(H):
                 mix(b, h)
 
-        pack_k(0)
-        pack_q(0)
-        quant_k(0)
+        pack_k(nc.vector.tensor_copy, 0)
+        pack_k(nc.scalar.copy, 1)
+        for r in range(PACK):
+            quant_k(r)
+        pack_q(nc.vector.tensor_copy, 0)
+        pack_q(nc.scalar.copy, 2)
+        pack_q(nc.scalar.copy, 3)
+        pack_q(nc.vector.tensor_copy, 1)
         quant_q(0)
-        pack_k(1)
-        quant_k(1)
         scores_exp(0)
-        mask_times_t(0)
-        pack_q(1)
-        weigh(0, 0)
         quant_q(1)
-        scores_exp(1)
+        mask_times_t(0)
+        mask_times_t(1)
+        mask_times_t(2)
+        quant_q(2)
+        mask_times_t(3)
+        quant_q(3)
         pack_v(0)
+        scores_exp(1)
         pack_v(1)
+        weigh(0, 0)
         weigh(0, 1)
         weigh(0, 2)
         quant_w(0, 0, 2)
         weigh(0, 3)
-        mask_times_t(1)
-        quant_w(0, 2, 2)
         weigh(1, 0)
-        pack_q(2)
-        weigh(1, 1)
-        quant_q(2)
+        quant_w(0, 2, 2)
         scores_exp(2)
+        pack_v(2)
+        pack_v(3)
+        weigh(1, 1)
         weigh(1, 2)
         quant_w(1, 0, 2)
-        pack_q(3)
         weigh(1, 3)
-        quant_q(3)
-        quant_v(0)
-        quant_w(1, 2, 2)
-        mask_times_t(2)
-        quant_v(1)
-        mix_block(0)
-        mix_block(1)
         weigh(2, 0)
-        invert(0, 0, H)
-        divide(0, 0, H)
-        weigh(2, 1)
-        invert(1, 0, H)
+        quant_w(1, 2, 2)
         scores_exp(3)
-        divide(1, 0, H)
+        weigh(2, 1)
+        quant_v(0)
         weigh(2, 2)
         quant_w(2, 0, 2)
         weigh(2, 3)
+        quant_v(1)
+        mix_block(0)
+        mix_block(1)
         weigh(3, 0)
         quant_w(2, 2, 2)
         mix_block(2)
+        invert(0, 0, H)
+        divide(0, 0, H)
+        invert(1, 0, H)
+        divide(1, 0, H)
         weigh(3, 1)
         invert(2, 0, H)
         divide(2, 0, H)

@@ -47,6 +47,11 @@ def tile_rows_mask_kernel(tc, qT, kT, t, v, mask, out):
             nc.sync.dma_start(out=raw[:], in_=rows[:, first : first + count, :])
             return raw
 
+        def load_q(half):
+            raw = tile("q_raw%d" % half, [P, PACK, 2 * QB], F32)
+            nc.sync.dma_start(out=raw[:], in_=q_rows[:, :, 2 * QB * half : 2 * QB * (half + 1)])
+            return raw
+
         def load_v(pair):
             raw = tile("v_raw%d" % pair, [P, 2, PACK * D], F32)
             nc.sync.dma_start(out=raw[:], in_=v_rows[:, 2 * pair : 2 * pair + 2, :])
@@ -55,9 +60,10 @@ def tile_rows_mask_kernel(tc, qT, kT, t, v, mask, out):
         t_sb = tile("t_sb", [P, PACK], F32)
         nc.scalar.dma_start(out=t_sb[:], in_=t.rearrange("(p r) o -> p (r o)", r=PACK))
         k_raw = load("k_raw", k_rows, 0, PACK)
-        q_raw = load("q_raw", q_rows, 0, PACK)
+        q_raw = [load_q(0)]
         m_first = load("m_raw0", m_rows, 0, 2)
         m_raw = [m_first[:, 0, :], m_first[:, 1, :], load("m_raw2", m_rows, 2, 1)[:, 0, :], load("m_raw3", m_rows, 3, 1)[:, 0, :]]
+        q_raw.append(load_q(1))
         v_raw = [load_v(0), load_v(1)]
 
         score_bank = [ps.tile([P, PACK, QB], F32, name="score%d" % h) for h in range(H)]
@@ -88,7 +94,7 @@ def tile_rows_mask_kernel(tc, qT, kT, t, v, mask, out):
         def pack_q(copy, b):
             copy(
                 out=q_bf[b][:].rearrange("p (c i) j -> p c j i", i=4),
-                in_=q_raw[:, :, QB * b : QB * (b + 1)].rearrange("p j (c i) -> p c j i", i=4),
+                in_=q_raw[b // 2][:, :, QB * (b % 2) : QB * (b % 2 + 1)].rearrange("p j (c i) -> p c j i", i=4),
             )
 
         def quant_q(b):
@@ -181,32 +187,32 @@ def tile_rows_mask_kernel(tc, qT, kT, t, v, mask, out):
 
         pack_k(nc.vector.tensor_copy, 0)
         pack_k(nc.scalar.copy, 1)
-        for r in range(PACK):
-            quant_k(r)
+        quant_k(0)
+        quant_k(1)
         pack_q(nc.vector.tensor_copy, 0)
-        pack_q(nc.scalar.copy, 2)
-        pack_q(nc.scalar.copy, 3)
-        pack_q(nc.vector.tensor_copy, 1)
+        pack_q(nc.scalar.copy, 1)
+        quant_k(2)
+        quant_k(3)
         quant_q(0)
         scores_exp(0)
+        for r in range(PACK):
+            mask_times_t(r)
         quant_q(1)
-        mask_times_t(0)
-        mask_times_t(1)
-        mask_times_t(2)
-        quant_q(2)
-        mask_times_t(3)
-        quant_q(3)
-        pack_v(0)
+        pack_q(nc.scalar.copy, 2)
         scores_exp(1)
-        pack_v(1)
         weigh(0, 0)
         weigh(0, 1)
+        pack_q(nc.vector.tensor_copy, 3)
         weigh(0, 2)
+        quant_q(2)
         quant_w(0, 0, 2)
         weigh(0, 3)
+        quant_q(3)
+        pack_v(0)
+        pack_v(1)
+        scores_exp(2)
         weigh(1, 0)
         quant_w(0, 2, 2)
-        scores_exp(2)
         pack_v(2)
         pack_v(3)
         weigh(1, 1)
@@ -228,13 +234,16 @@ def tile_rows_mask_kernel(tc, qT, kT, t, v, mask, out):
         quant_w(2, 2, 2)
         mix_block(2)
         invert(0, 0, H)
-        divide(0, 0, H)
-        invert(1, 0, H)
-        divide(1, 0, H)
+        divide(0, 0, 2)
+        divide(0, 2, 2)
         weigh(3, 1)
-        invert(2, 0, H)
-        divide(2, 0, H)
+        invert(1, 0, H)
+        divide(1, 0, 2)
+        divide(1, 2, 2)
         weigh(3, 2)
+        invert(2, 0, H)
+        divide(2, 0, 2)
+        divide(2, 2, 2)
         quant_w(3, 0, 2)
         mix(3, 0)
         mix(3, 1)

from contextlib import ExitStack

import concourse.mybir as mybir

H, D, NQ, N = 4, 128, 512, 512
FLOPS = 2 * 2 * H * D * NQ * N

F32 = mybir.dt.float32
BF16 = mybir.dt.bfloat16
U32 = mybir.dt.uint32
U8 = mybir.dt.uint8
FP8X4 = mybir.dt.float8_e4m3fn_x4
ACT = mybir.ActivationFunctionType
ALU = mybir.AluOpType

P = 128
PACK = 4
ROWS = 32
QB = 128
BLOCKS = NQ // QB


def tile_rows_mask_kernel(tc, qT, kT, t, v, mask, out):
    nc = tc.nc
    with ExitStack() as ctx:
        sb = ctx.enter_context(tc.tile_pool(name="sb", bufs=1))
        ps = ctx.enter_context(tc.psum_pool(name="ps", bufs=1))
        ctx.enter_context(tc.manual_schedule())

        def tile(name, shape, dtype):
            return sb.tile(shape, dtype, name=name, align_bytes=64)

        def mx_tiles(name, words):
            return tile(name + "_codes", [P, words], U32), tile(name + "_scales", [P, words], U8)

        def quantize(mx, first, words, values):
            cols = slice(first, first + words)
            nc.vector.quantize_mx(out=mx[0][:, cols].bitcast(FP8X4), scales=mx[1][:, cols], in_=values)

        q_rows = qT.rearrange("h (p j) n -> (h p) j n", j=PACK)
        k_rows = kT.rearrange("h (p j) n -> (h p) j n", j=PACK)
        m_rows = mask.rearrange("(p r) n -> p r n", r=PACK)
        v_rows = v.rearrange("h (p r) e -> p h (r e)", r=PACK)

        def load(name, rows, first, count):
            raw = tile(name, [P, count, NQ], F32)
            nc.sync.dma_start(out=raw[:], in_=rows[:, first : first + count, :])
            return raw

        def load_q(half):
            raw = tile("q_raw%d" % half, [P, PACK, 2 * QB], F32)
            nc.sync.dma_start(out=raw[:], in_=q_rows[:, :, 2 * QB * half : 2 * QB * (half + 1)])
            return raw

        def load_v(pair):
            raw = tile("v_raw%d" % pair, [P, 2, PACK * D], F32)
            nc.sync.dma_start(out=raw[:], in_=v_rows[:, 2 * pair : 2 * pair + 2, :])
            return raw

        t_sb = tile("t_sb", [P, PACK], F32)
        nc.scalar.dma_start(out=t_sb[:], in_=t.rearrange("(p r) o -> p (r o)", r=PACK))
        k_raw = load("k_raw", k_rows, 0, PACK)
        q_raw = [load_q(0)]
        m_first = load("m_raw0", m_rows, 0, 2)
        m_raw = [m_first[:, 0, :], m_first[:, 1, :], load("m_raw2", m_rows, 2, 1)[:, 0, :], load("m_raw3", m_rows, 3, 1)[:, 0, :]]
        q_raw.append(load_q(1))
        v_raw = [load_v(0), load_v(1)]

        score_bank = [ps.tile([P, PACK, QB], F32, name="score%d" % h) for h in range(H)]
        y_bank = [ps.tile([P, H, D], F32, name="y%d" % b) for b in range(BLOCKS)]

        k_mx = [mx_tiles("k%d" % r, P) for r in range(PACK)]
        q_mx = [mx_tiles("q%d" % b, QB) for b in range(BLOCKS)]
        v_mx = [mx_tiles("v%d" % pair, 2 * D) for pair in range(2)]
        k_bf = [tile("k_bf%d" % half, [P, 2, P, PACK], BF16) for half in range(2)]
        q_bf = [tile("q_bf%d" % b, [P, QB, PACK], BF16) for b in range(BLOCKS)]
        v_bf = [tile("v_bf%d" % pair, [P, 2, D, PACK], BF16) for pair in range(2)]
        mt = tile("mt", [P, PACK, NQ], F32)
        p_sb = {(b, h): tile("p%d%d" % (b, h), [P, PACK * QB], F32) for b in range(BLOCKS) for h in range(H)}
        w_bf = {(b, pair): tile("w%d%d" % (b, pair), [P, 2, PACK * QB], BF16) for b in range(BLOCKS) for pair in range(2)}
        w_mx = {(b, pair): mx_tiles("w%d%d" % (b, pair), 2 * QB) for b in range(BLOCKS) for pair in range(2)}
        inv = [tile("inv%d" % b, [P, H], F32) for b in range(BLOCKS)]
        res = [tile("res%d" % b, [P, H, D], F32) for b in range(BLOCKS)]

        def pack_k(copy, half):
            copy(
                out=k_bf[half][:].rearrange("p r s j -> p s j r"),
                in_=k_raw[:].rearrange("p j (s r) -> p s j r", r=PACK)[:, :, :, 2 * half : 2 * half + 2],
            )

        def quant_k(r):
            quantize(k_mx[r], 0, P, k_bf[r // 2][:, r % 2].rearrange("p s j -> p (s j)"))

        def pack_q(copy, b):
            copy(
                out=q_bf[b][:].rearrange("p (c i) j -> p c j i", i=4),
                in_=q_raw[b // 2][:, :, QB * (b % 2) : QB * (b % 2 + 1)].rearrange("p j (c i) -> p c j i", i=4),
            )

        def quant_q(b):
            quantize(q_mx[b], 0, QB, q_bf[b][:].rearrange("p n j -> p (n j)"))

        def pack_v(h):
            nc.scalar.copy(
                out=v_bf[h // 2][:, h % 2].rearrange("p (c i) r -> p c r i", i=4),
                in_=v_raw[h // 2][:, h % 2, :].rearrange("p (r c i) -> p c r i", r=PACK, i=4),
            )

        def quant_v(pair):
            quantize(v_mx[pair], 0, 2 * D, v_bf[pair][:].rearrange("p h e r -> p (h e r)"))

        def mask_times_t(r):
            nc.vector.tensor_scalar(out=mt[:, r, :], in0=m_raw[r], scalar1=t_sb[:, r : r + 1], scalar2=None, op0=ALU.mult)

        def scores(b, h):
            rows = slice(ROWS * h, ROWS * (h + 1))
            for r in range(PACK):
                nc.tensor.matmul_mx(
                    out=score_bank[h][:, r, :],
                    lhsT=k_mx[r][0][rows, :].bitcast(FP8X4),
                    lhsT_scale=k_mx[r][1][rows, :],
                    rhs=q_mx[b][0][rows, :].bitcast(FP8X4),
                    rhs_scale=q_mx[b][1][rows, :],
                    start=True,
                    stop=True,
                )

        def exp(b, h):
            nc.scalar.activation(
                out=p_sb[b, h][:].rearrange("p (c r i) -> p c r i", r=PACK, i=2),
                in_=score_bank[h][:].rearrange("p r (c i) -> p c r i", i=2),
                func=ACT.Exp,
            )

        def weigh(b, h):
            nc.vector.tensor_tensor(
                out=w_bf[b, h // 2][:, h % 2, :].rearrange("p (c i r) -> p c r i", r=PACK, i=2),
                in0=p_sb[b, h][:].rearrange("p (c r i) -> p c r i", r=PACK, i=2),
                in1=mt[:, :, QB * b : QB * (b + 1)].rearrange("p r (c i) -> p c r i", i=2),
                op=ALU.mult,
            )

        def quant_w(b, first, count):
            values = w_bf[b, first // 2][:].rearrange("p h n -> p (h n)")
            start = (first % 2) * PACK * QB
            quantize(w_mx[b, first // 2], (first % 2) * QB, count * QB, values[:, start : start + count * PACK * QB])

        def y_of(b, h):
            bank = (b + max(h - 1, 0)) % BLOCKS if b == BLOCKS - 1 else b
            return y_bank[bank][:, h, :]

        def mix(b, h):
            cols = slice((h % 2) * QB, (h % 2 + 1) * QB)
            nc.tensor.matmul_mx(
                out=y_of(b, h),
                lhsT=w_mx[b, h // 2][0][:, cols].bitcast(FP8X4),
                lhsT_scale=w_mx[b, h // 2][1][:, cols],
                rhs=v_mx[h // 2][0][:, cols].bitcast(FP8X4),
                rhs_scale=v_mx[h // 2][1][:, cols],
                start=True,
                stop=True,
            )

        def invert(b, first, count):
            if count == 1:
                src = y_of(b, first)[:, D - 1 : D]
            else:
                src = y_bank[b][:, first : first + count, D - 1]
            nc.vector.reciprocal(out=inv[b][:, first : first + count], in_=src)

        def divide(b, first, count):
            for h in range(first, first + count):
                nc.scalar.activation(out=res[b][:, h, :], in_=y_of(b, h), func=ACT.Copy, scale=inv[b][:, h : h + 1])
            heads = slice(first, first + count)
            nc.sync.dma_start(
                out=out[heads, QB * b : QB * (b + 1), :].rearrange("h q e -> q h e"), in_=res[b][:, heads, :]
            )

        def scores_exp(b):
            for h in range(H):
                scores(b, h)
                exp(b, h)

        def mix_block(b):
            for h in range(H):
                mix(b, h)

        pack_k(nc.vector.tensor_copy, 0)
        pack_k(nc.scalar.copy, 1)
        quant_k(0)
        quant_k(1)
        pack_q(nc.vector.tensor_copy, 0)
        pack_q(nc.scalar.copy, 1)
        quant_k(2)
        quant_k(3)
        quant_q(0)
        scores_exp(0)
        for r in range(PACK):
            mask_times_t(r)
        quant_q(1)
        pack_q(nc.scalar.copy, 2)
        scores_exp(1)
        weigh(0, 0)
        weigh(0, 1)
        pack_q(nc.vector.tensor_copy, 3)
        weigh(0, 2)
        quant_q(2)
        quant_w(0, 0, 2)
        weigh(0, 3)
        quant_q(3)
        pack_v(0)
        pack_v(1)
        scores_exp(2)
        weigh(1, 0)
        quant_w(0, 2, 2)
        pack_v(2)
        pack_v(3)
        weigh(1, 1)
        weigh(1, 2)
        quant_w(1, 0, 2)
        weigh(1, 3)
        weigh(2, 0)
        quant_w(1, 2, 2)
        scores_exp(3)
        weigh(2, 1)
        quant_v(0)
        weigh(2, 2)
        quant_w(2, 0, 2)
        weigh(2, 3)
        quant_v(1)
        mix_block(0)
        mix_block(1)
        weigh(3, 0)
        quant_w(2, 2, 2)
        mix_block(2)
        invert(0, 0, H)
        divide(0, 0, 2)
        divide(0, 2, 2)
        weigh(3, 1)
        invert(1, 0, H)
        divide(1, 0, 2)
        divide(1, 2, 2)
        weigh(3, 2)
        invert(2, 0, H)
        divide(2, 0, 2)
        divide(2, 2, 2)
        quant_w(3, 0, 2)
        mix(3, 0)
        mix(3, 1)
        weigh(3, 3)
        quant_w(3, 2, 1)
        mix(3, 2)
        invert(3, 0, 2)
        divide(3, 0, 2)
        quant_w(3, 3, 1)
        mix(3, 3)
        invert(3, 2, 1)
        divide(3, 2, 1)
        invert(3, 3, 1)
        divide(3, 3, 1)
